import numpy as np
import ml_dtypes


def mxq(x, axis, fmt="e4m3"):
    dtype, down = {"e4m3": (ml_dtypes.float8_e4m3fn, 7), "e5m2": (ml_dtypes.float8_e5m2, 14)}[fmt]
    v = np.moveaxis(np.asarray(x, np.float32).astype(ml_dtypes.bfloat16).astype(np.float64), axis, -1)
    blocks = v.reshape(v.shape[:-1] + (-1, 32))
    amax = np.abs(blocks).max(-1, keepdims=True)
    byte = np.maximum(np.where(amax > 0, np.frexp(amax)[1] - 1 + 127, 0) - down, 1)
    scale = np.exp2(byte - 127.0)
    codes = (blocks / scale).astype(np.float32).astype(dtype).astype(np.float64)
    return np.moveaxis((codes * scale).reshape(v.shape), -1, axis)


WIDE = False


def mx_kscale(k):
    if not WIDE:
        return np.ones(k)
    levels = np.array([10, -10, 5, -5, 0])
    if k % 512:
        return np.exp2(np.random.permutation(np.resize(levels, k // 32))).repeat(32)
    a = np.empty((k // 512, 16))
    for p in range(k // 512):
        a[p, :8] = np.random.permutation(np.resize(levels, 8))
        for g in range(8):
            far = levels[np.abs(levels - a[p, g]) >= 10]
            a[p, g + 8] = far[np.random.randint(len(far))]
    return np.exp2(a.ravel()).repeat(32)


BF16 = ml_dtypes.bfloat16


def bf(x):
    return np.asarray(x, np.float32).astype(BF16)


def f64(x):
    return np.asarray(x).astype(np.float64)


B, HH, WW, D, F, KH, KW = 1, 32, 32, 512, 1024, 3, 3
F2 = 2 * F


def silu(z):
    return z / (1.0 + np.exp(-z))


def depthwise_corr(u, wd):
    rows, cols = u.shape[1], u.shape[2]
    ph, pw = KH // 2, KW // 2
    upad = np.pad(u, ((0, 0), (ph, ph), (pw, pw), (0, 0)))
    c = np.zeros_like(u)
    for r in range(KH):
        band = upad[:, r:r + rows, :, :]
        for t in range(KW):
            c = c + wd[r, t] * band[:, :, t:t + cols, :]
    return c


def draw0():
    s, t = mx_kscale(D), mx_kscale(F)
    return {"x": bf(np.random.standard_normal((B, HH, WW, D)) * s),
            "w1": bf(np.random.standard_normal((D, F2)) / np.sqrt(D) / s[:, None]),
            "b1": bf(np.random.standard_normal(F2) * 0.3),
            "wd": bf(np.random.standard_normal((KH, KW, F2)) * 0.5),
            "gain": bf((1.0 + 0.1 * np.random.standard_normal(F)) * t),
            "w2": bf(np.random.standard_normal((F, D)) * 2.0 / np.sqrt(F) / t[:, None])}


def core(x, w1, b1, wd, gain, w2):
    f = gain.shape[0]
    h = (mxq(f64(x), 3, "e4m3") @ mxq(f64(w1), 0, "e4m3")) + f64(b1)
    u = silu(h)
    c = depthwise_corr(u, f64(wd))
    ca = c[..., :f]
    cb = c[..., f:]
    g = f64(gain) * ca * silu(cb)
    return mxq(g, 3, "e4m3") @ mxq(f64(w2), 0, "e4m3")


def e4m3fn_bytes(y):
    return np.clip(np.asarray(y, np.float64), -448.0, 448.0).astype(np.float32).astype(ml_dtypes.float8_e4m3fn).view(np.uint8)


def e4m3fn_values(b):
    return np.asarray(b, np.uint8).view(ml_dtypes.float8_e4m3fn).astype(np.float64)


def setup_inputs():
    d = draw0()
    x0 = np.asarray(d['w1']).astype(np.float64)
    s = (np.max(np.abs(x0), axis=(1,), keepdims=True) / 448.0).astype(np.float32)
    out = {}
    for k, v in d.items():
        if k == 'w1':
            out['w1_bytes'] = e4m3fn_bytes(x0 / s.astype(np.float64))
            out['w1_scale'] = s
        else:
            out[k] = v
    return out


def reference(x, w1_bytes, w1_scale, b1, wd, gain, w2):
    return core(x, e4m3fn_values(w1_bytes) * w1_scale.astype(np.float64), b1, wd, gain, w2)

@@ -1,0 +1,354 @@
+from contextlib import ExitStack
+
+import concourse.mybir as mybir
+from concourse.masks import make_identity
+
+P = 128
+TOK = 1024
+GRID = 32
+D = 512
+F = 1024
+F2 = 2 * F
+
+F32 = mybir.dt.float32
+BF16 = mybir.dt.bfloat16
+U32 = mybir.dt.uint32
+U8 = mybir.dt.uint8
+FP8 = mybir.dt.float8_e4m3fn
+X4 = mybir.dt.float8_e4m3fn_x4
+ACT = mybir.ActivationFunctionType
+ALU = mybir.AluOpType
+
+FLOPS = 2 * TOK * D * F2 + 2 * TOK * F * D + 2 * 9 * TOK * F2 + 3 * TOK * F
+
+N_TILES = F2 // P
+PITCH = 40
+COL0 = 4
+MERGES = 2
+
+
+def tile_sanamixffndepthwiseglu_kernel(tc, x, w1_bytes, w1_scale, b1, wd, gain, w2, out):
+    nc = tc.nc
+    with ExitStack() as ctx:
+        const = ctx.enter_context(tc.tile_pool(name="const", bufs=1))
+        work = ctx.enter_context(tc.tile_pool(name="work", bufs=2))
+        psum = ctx.enter_context(tc.psum_pool(name="psum", bufs=1))
+        ctx.enter_context(tc.manual_schedule())
+
+        def bank(i):
+            return psum.tile([P, 512], F32, name="bank%d" % i, tag="bank%d" % i)
+
+        x_view = x.rearrange("b h w d -> (b h w) d").rearrange("(q j p) d -> q p j d", j=2, p=P)
+        w1_view = w1_bytes.rearrange("(p t) n -> p t n", t=4)
+        w2_view = w2.rearrange("(q p t) n -> q p t n", p=P, t=4)
+
+        ident = const.tile([P, P], F32, name="ident")
+        make_identity(nc, ident[:])
+        u_bufs = []
+        for i in range(3):
+            u = const.tile([P, GRID + 2, PITCH], F32, name="u%d" % i)
+            nc.gpsimd.memset(u[:], 0.0)
+            u_bufs.append(u)
+
+        praw = const.tile([P, 2, P], BF16, name="praw")
+        nc.vector.memset(praw[:, 1, :], 0.0)
+        warm = const.tile([P, 1], F32, name="warm")
+        nc.vector.memset(warm[:], 0.0)
+        nc.scalar.activation(out=warm[:], in_=warm[:], func=ACT.Silu)
+
+        x_sb = [const.tile([P, 2, D], BF16, name="x_sb%d" % q) for q in range(4)]
+        w1_sb = [const.tile([P, 4, 512], U8, name="w1_sb%d" % c) for c in range(4)]
+        w2_sb = [const.tile([P, 4, D], BF16, name="w2_sb%d" % q) for q in range(2)]
+        scale_sb = const.tile([P, 4], F32, name="scale_sb")
+
+        def load_x(q):
+            nc.sync.dma_start(out=x_sb[q][:], in_=x_view[q])
+
+        def load_w1(c):
+            nc.sync.dma_start(out=w1_sb[c][:], in_=w1_view[:, :, 512 * c : 512 * (c + 1)])
+
+        nc.scalar.dma_start(out=scale_sb[:], in_=w1_scale.rearrange("(p t) o -> p (t o)", t=4))
+        wd_rows = wd.rearrange("r t (c p) -> (r t c) p", p=P)
+        nc.scalar.dma_start(out=praw[:, 0, :], in_=wd_rows[0:128, :])
+        nc.scalar.dma_start(out=praw[0:16, 1, :], in_=wd_rows[128:144, :])
+        nc.scalar.dma_start(out=praw[16:32, 1, :], in_=b1.rearrange("(c p) -> c p", p=P))
+        nc.scalar.dma_start(out=praw[32:40, 1, :], in_=gain.rearrange("(c p) -> c p", p=P))
+        load_w1(2)
+        load_x(0)
+        load_x(1)
+        load_x(2)
+        load_x(3)
+        load_w1(0)
+        load_w1(3)
+        load_w1(1)
+        for q in range(2):
+            nc.sync.dma_start(out=w2_sb[q][:], in_=w2_view[q])
+
+        w1_codes = [const.tile([P, 512], U32, name="w1_codes%d" % c, align_bytes=64) for c in range(4)]
+        w1_scales = [const.tile([P, 512], U8, name="w1_scales%d" % c, align_bytes=64) for c in range(4)]
+        planes = {}
+        grouped = {}
+
+        def widen(c, t, engine):
+            if t == 0:
+                planes[c] = work.tile([P, 4, 512], BF16, name="planes", tag="planes", align_bytes=64)
+            src = w1_sb[c][:, t, :].bitcast(FP8)
+            dst = planes[c][:, t, :]
+            if engine == "s":
+                nc.scalar.activation(out=dst, in_=src, func=ACT.Copy, scale=scale_sb[:, t : t + 1])
+            else:
+                nc.vector.tensor_scalar(out=dst, in0=src, scalar1=scale_sb[:, t : t + 1], scalar2=None, op0=ALU.mult)
+
+        def interleave(key, src, engine):
+            dst = work.tile([P, 512, 4], BF16, name="grouped", tag="grouped", align_bytes=64)
+            grouped[key] = dst
+            view = src.rearrange("p t n -> p n t")
+            if engine == "s":
+                nc.scalar.copy(out=dst[:], in_=view)
+            else:
+                nc.vector.tensor_copy(out=dst[:], in_=view)
+
+        def quantise(key, codes, scales):
+            nc.vector.quantize_mx(out=codes.bitcast(X4), scales=scales, in_=grouped[key][:].rearrange("p n t -> p (n t)"))
+
+        x_codes = const.tile([P, TOK], U32, name="x_codes", align_bytes=64)
+        x_scales = const.tile([P, TOK], U8, name="x_scales", align_bytes=64)
+        pair_tiles = {}
+
+        def word_transposes(key, sources, b):
+            tx = bank(b)
+            for j in range(2):
+                words = sources[j].bitcast(F32)
+                for h in range(2):
+                    col = (2 * j + h) * P
+                    nc.tensor.transpose(tx[:, col : col + P], words[:, h:256:2], ident[:])
+            pair_tiles[key] = tx
+
+        def word_copy(key, engine):
+            dst = work.tile([P, 256, 4], BF16, name="pairs", tag="pairs", bufs=4, align_bytes=64)
+            o = dst[:].rearrange("p n t -> p (n t)").bitcast(F32).rearrange("p (j r h) -> p j r h", j=2, h=2)
+            i = pair_tiles[key][:].rearrange("p (j h r) -> p j r h", j=2, h=2)
+            if engine == "s":
+                nc.scalar.copy(out=o, in_=i)
+            else:
+                nc.vector.tensor_copy(out=o, in_=i)
+            grouped[key] = dst
+
+        pf = const.tile([P, 2, P], F32, name="pf")
+        nc.vector.tensor_copy(out=pf[:], in_=praw[:])
+        pbank = bank(2)
+        for h in range(2):
+            nc.tensor.transpose(pbank[:, P * h : P * (h + 1)], pf[:, h, :], ident[:])
+        par = const.tile([P, 2 * P], F32, name="par")
+        nc.vector.tensor_copy(out=par[:], in_=pbank[:, 0 : 2 * P])
+        wg = const.tile([P, 9, 8], F32, name="wg")
+        for tap in range(9):
+            nc.gpsimd.tensor_tensor(out=wg[:, tap, :], in0=par[:, 16 * tap : 16 * tap + 8], in1=par[:, 160:168], op=ALU.mult)
+
+        def weight(tap, c):
+            if c < 8:
+                return wg[:, tap, c : c + 1]
+            return par[:, 16 * tap + c : 16 * tap + c + 1]
+
+        def bias(c):
+            return par[:, 144 + c : 145 + c]
+
+        for t in range(4):
+            widen(2, t, "s")
+        for q in range(4):
+            word_transposes("x%d" % q, [x_sb[q][:, j, :] for j in range(2)], 4 + q)
+        interleave("w2c", planes[2][:], "v")
+        word_copy("x0", "v")
+        quantise("w2c", w1_codes[2][:], w1_scales[2][:])
+        word_copy("x1", "s")
+        word_copy("x2", "v")
+        for q in range(2):
+            quantise("x%d" % q, x_codes[:, 256 * q : 256 * (q + 1)], x_scales[:, 256 * q : 256 * (q + 1)])
+        word_copy("x3", "s")
+        for q in range(2, 4):
+            quantise("x%d" % q, x_codes[:, 256 * q : 256 * (q + 1)], x_scales[:, 256 * q : 256 * (q + 1)])
+
+        h_banks = {}
+        c_banks = {}
+        groups = {}
+        gate = {}
+        g_sb = const.tile([P, 8, F], BF16, name="g_sb", align_bytes=64)
+        g_codes = [const.tile([P, TOK], U32, name="g_codes%d" % q, align_bytes=64) for q in range(2)]
+        g_scales = [const.tile([P, TOK], U8, name="g_scales%d" % q, align_bytes=64) for q in range(2)]
+
+        def channel_tile(i):
+            return i // 2 + (8 if i % 2 == 0 else 0)
+
+        def stage1(i):
+            c = channel_tile(i)
+            lo = P * (c % 4)
+            h_banks[i] = [bank(0), bank(1)]
+            for hh in range(2):
+                nc.tensor.matmul_mx(
+                    out=h_banks[i][hh][:],
+                    lhsT=w1_codes[c // 4][:, lo : lo + P].bitcast(X4),
+                    lhsT_scale=w1_scales[c // 4][:, lo : lo + P],
+                    rhs=x_codes[:, 512 * hh : 512 * (hh + 1)].bitcast(X4),
+                    rhs_scale=x_scales[:, 512 * hh : 512 * (hh + 1)],
+                    start=True,
+                    stop=True,
+                )
+
+        def silu_u(i):
+            c = channel_tile(i)
+            u = u_bufs[i % 3]
+            for hh in range(2):
+                nc.scalar.activation(
+                    out=u[:, 1 + 16 * hh : 17 + 16 * hh, COL0 : COL0 + GRID],
+                    in_=h_banks[i][hh][:].rearrange("p (r c) -> p r c", c=GRID),
+                    func=ACT.Silu,
+                    bias=bias(c),
+                    scale=1.0,
+                )
+
+        def taps_of(i):
+            u = u_bufs[i % 3]
+            c = channel_tile(i)
+
+            def src(tap):
+                r, t = divmod(tap, 3)
+                return u[:, r : r + GRID, COL0 - 1 + t : COL0 - 1 + t + GRID]
+
+            return src, c
+
+        def n_scalar(i):
+            return 3 if i % 2 == 0 else 4
+
+        def products(i):
+            src, c = taps_of(i)
+            n = 9 - MERGES
+            tiles = [work.tile([P, TOK], F32, name="grp%d" % k, tag="grp%d" % k) for k in range(n)]
+            views = [t[:].rearrange("p (r c) -> p r c", c=GRID) for t in tiles]
+            groups[i] = tiles
+            ns = n_scalar(i)
+            for k in range(n - ns, n):
+                tap = k + MERGES
+                nc.scalar.activation(out=views[k], in_=src(tap), func=ACT.Copy, scale=weight(tap, c))
+            for k in range(MERGES):
+                nc.vector.tensor_scalar(out=views[k], in0=src(2 * k), scalar1=weight(2 * k, c), scalar2=None, op0=ALU.mult)
+            for k in range(MERGES):
+                tap = 2 * k + 1
+                nc.vector.scalar_tensor_tensor(out=views[k], in0=src(tap), scalar=weight(tap, c), in1=views[k], op0=ALU.mult, op1=ALU.add)
+            for k in range(MERGES, n - ns):
+                tap = k + MERGES
+                nc.vector.tensor_scalar(out=views[k], in0=src(tap), scalar1=weight(tap, c), scalar2=None, op0=ALU.mult)
+
+        def conv(i):
+            base = 2 if i % 2 == 0 else 4
+            c_banks[i] = [bank(base), bank(base + 1)]
+            tiles = groups[i]
+            for hh in range(2):
+                for j in range(4):
+                    tok = (4 * hh + j) * P
+                    for k in range(len(tiles)):
+                        nc.tensor.matmul(
+                            out=c_banks[i][hh][:, P * j : P * (j + 1)],
+                            lhsT=tiles[k][:, tok : tok + P],
+                            rhs=ident[:],
+                            is_transpose=True,
+                            start=(k == 0),
+                            stop=(k == len(tiles) - 1),
+                        )
+
+        def epilogue(i):
+            if i % 2 == 0:
+                gate[i // 2] = []
+                for hh in range(2):
+                    s = work.tile([P, 512], F32, name="gate%d" % hh, tag="gate%d" % hh)
+                    nc.scalar.activation(out=s[:], in_=c_banks[i][hh][:], func=ACT.Silu)
+                    gate[i // 2].append(s)
+            else:
+                k = i // 2
+                for hh in range(2):
+                    nc.vector.tensor_tensor(
+                        out=g_sb[:, 4 * hh : 4 * hh + 4, P * k : P * (k + 1)],
+                        in0=c_banks[i][hh][:].rearrange("p (j c) -> p j c", c=P),
+                        in1=gate[k][hh][:].rearrange("p (j c) -> p j c", c=P),
+                        op=ALU.mult,
+                    )
+
+        def g_transposes(jj, q, b):
+            word_transposes("g%d_%d" % (jj, q), [g_sb[:, 2 * jj + j, 512 * q : 512 * (q + 1)] for j in range(2)], b)
+
+        def g_quantise(jj, q):
+            quantise("g%d_%d" % (jj, q), g_codes[q][:, 256 * jj : 256 * (jj + 1)], g_scales[q][:, 256 * jj : 256 * (jj + 1)])
+
+        w2_codes = [const.tile([P, D], U32, name="w2_codes%d" % q, align_bytes=64) for q in range(2)]
+        w2_scales = [const.tile([P, D], U8, name="w2_scales%d" % q, align_bytes=64) for q in range(2)]
+
+        stage1(0)
+        silu_u(0)
+        for t in range(4):
+            widen(0, t, "v")
+        interleave("w0c", planes[0][:], "v")
+        quantise("w0c", w1_codes[0][:], w1_scales[0][:])
+        products(0)
+        stage1(1)
+        silu_u(1)
+        for i in range(N_TILES):
+            if i + 2 < N_TILES:
+                stage1(i + 2)
+            if 9 <= i and i % 2 == 1:
+                g_transposes((i - 9) // 2, 0, 6 + ((i - 9) // 2) % 2)
+            if i >= 1:
+                epilogue(i - 1)
+            if 10 <= i and i % 2 == 0:
+                g_quantise((i - 10) // 2, 0)
+            if i + 2 < N_TILES:
+                silu_u(i + 2)
+            if i + 1 < N_TILES:
+                products(i + 1)
+            if i == 1:
+                for t in range(4):
+                    widen(3, t, "s")
+            if i == 2:
+                interleave("w3c", planes[3][:], "v")
+            if i == 3:
+                quantise("w3c", w1_codes[3][:], w1_scales[3][:])
+                for t in range(4):
+                    widen(1, t, "s")
+            if i == 4:
+                interleave("w1c", planes[1][:], "v")
+            if i == 5:
+                quantise("w1c", w1_codes[1][:], w1_scales[1][:])
+            if i == 6 or i == 8:
+                interleave("v%d" % ((i - 6) // 2), w2_sb[(i - 6) // 2][:], "v")
+            if i == 7 or i == 9:
+                q = (i - 7) // 2
+                quantise("v%d" % q, w2_codes[q][:], w2_scales[q][:])
+            if 9 <= i and i % 2 == 1:
+                word_copy("g%d_%d" % ((i - 9) // 2, 0), "s")
+            conv(i)
+        epilogue(N_TILES - 1)
+        g_quantise(3, 0)
+
+        out_view = out.rearrange("b h w d -> (b h w) d")
+        for jj in range(4):
+            g_transposes(jj, 1, 4 + jj)
+        for jj in range(4):
+            word_copy("g%d_1" % jj, "s" if jj % 2 else "v")
+        for jj in range(4):
+            g_quantise(jj, 1)
+        for j in range(8):
+            acc = bank(j % 4)
+            for q in range(2):
+                nc.tensor.matmul_mx(
+                    out=acc[:],
+                    lhsT=g_codes[q][:, P * j : P * (j + 1)].bitcast(X4),
+                    lhsT_scale=g_scales[q][:, P * j : P * (j + 1)],
+                    rhs=w2_codes[q][:].bitcast(X4),
+                    rhs_scale=w2_scales[q][:],
+                    start=(q == 0),
+                    stop=(q == 1),
+                )
+            res = work.tile([P, D], F32, name="res", tag="res", bufs=4)
+            if j % 2 == 0:
+                nc.scalar.copy(out=res[:], in_=acc[:])
+            else:
+                nc.vector.tensor_copy(out=res[:], in_=acc[:])
+            nc.sync.dma_start(out=out_view[P * j : P * (j + 1), :], in_=res[:])

@@ -22,9 +22,10 @@ ALU = mybir.AluOpType
 FLOPS = 2 * TOK * D * F2 + 2 * TOK * F * D + 2 * 9 * TOK * F2 + 3 * TOK * F
 
 N_TILES = F2 // P
+WIDEN = "vvvv"
 PITCH = 40
 COL0 = 4
-MERGES = 2
+CONFIG = ((2, 3), (2, 4))
 
 
 def tile_sanamixffndepthwiseglu_kernel(tc, x, w1_bytes, w1_scale, b1, wd, gain, w2, out):
@@ -56,8 +57,8 @@ def tile_sanamixffndepthwiseglu_kernel(tc, x, w1_bytes, w1_scale, b1, wd, gain, 
         nc.vector.memset(warm[:], 0.0)
         nc.scalar.activation(out=warm[:], in_=warm[:], func=ACT.Silu)
 
-        x_sb = [const.tile([P, 2, D], BF16, name="x_sb%d" % q) for q in range(4)]
-        w1_sb = [const.tile([P, 4, 512], U8, name="w1_sb%d" % c) for c in range(4)]
+        x_sb = [const.tile([P, 2, D], BF16, name="x_sb%d" % q, tag="io%d" % q) for q in range(4)]
+        w1_sb = [const.tile([P, 4, 512], U8, name="w1_sb%d" % c, tag="io%d" % (4 + c)) for c in range(4)]
         w2_sb = [const.tile([P, 4, D], BF16, name="w2_sb%d" % q) for q in range(2)]
         scale_sb = const.tile([P, 4], F32, name="scale_sb")
 
@@ -73,8 +74,8 @@ def tile_sanamixffndepthwiseglu_kernel(tc, x, w1_bytes, w1_scale, b1, wd, gain, 
         nc.scalar.dma_start(out=praw[0:16, 1, :], in_=wd_rows[128:144, :])
         nc.scalar.dma_start(out=praw[16:32, 1, :], in_=b1.rearrange("(c p) -> c p", p=P))
         nc.scalar.dma_start(out=praw[32:40, 1, :], in_=gain.rearrange("(c p) -> c p", p=P))
-        load_w1(2)
         load_x(0)
+        load_w1(2)
         load_x(1)
         load_x(2)
         load_x(3)
@@ -84,29 +85,42 @@ def tile_sanamixffndepthwiseglu_kernel(tc, x, w1_bytes, w1_scale, b1, wd, gain, 
         for q in range(2):
             nc.sync.dma_start(out=w2_sb[q][:], in_=w2_view[q])
 
-        w1_codes = [const.tile([P, 512], U32, name="w1_codes%d" % c, align_bytes=64) for c in range(4)]
-        w1_scales = [const.tile([P, 512], U8, name="w1_scales%d" % c, align_bytes=64) for c in range(4)]
+        chunks = {"b0": (2, 0, 256), "b1": (2, 256, 256), "b2": (3, 0, 512), "a0": (0, 0, 256), "a1": (0, 256, 256), "a2": (1, 0, 512)}
+        w1_codes = {}
+        w1_scales = {}
+        for name in chunks:
+            width = chunks[name][2]
+            w1_codes[name] = const.tile([P, width], U32, name="w1_codes_" + name, align_bytes=64)
+            w1_scales[name] = const.tile([P, width], U8, name="w1_scales_" + name, align_bytes=64)
         planes = {}
         grouped = {}
 
-        def widen(c, t, engine):
+        def widen(name, t, engine):
+            c, lo, width = chunks[name]
             if t == 0:
-                planes[c] = work.tile([P, 4, 512], BF16, name="planes", tag="planes", align_bytes=64)
-            src = w1_sb[c][:, t, :].bitcast(FP8)
-            dst = planes[c][:, t, :]
+                planes[name] = work.tile([P, 4, width], BF16, name="planes%d" % width, tag="planes%d" % width, align_bytes=64)
+            src = w1_sb[c][:, t, lo : lo + width].bitcast(FP8)
+            dst = planes[name][:, t, :]
             if engine == "s":
                 nc.scalar.activation(out=dst, in_=src, func=ACT.Copy, scale=scale_sb[:, t : t + 1])
             else:
                 nc.vector.tensor_scalar(out=dst, in0=src, scalar1=scale_sb[:, t : t + 1], scalar2=None, op0=ALU.mult)
 
         def interleave(key, src, engine):
-            dst = work.tile([P, 512, 4], BF16, name="grouped", tag="grouped", align_bytes=64)
+            width = src.shape[2]
+            dst = work.tile([P, width, 4], BF16, name="grouped%d" % width, tag="grouped%d" % width, align_bytes=64)
             grouped[key] = dst
             view = src.rearrange("p t n -> p n t")
             if engine == "s":
                 nc.scalar.copy(out=dst[:], in_=view)
             else:
                 nc.vector.tensor_copy(out=dst[:], in_=view)
+
+        def w1_interleave(name, engine):
+            interleave(name, planes[name][:], engine)
+
+        def w1_quantise(name):
+            quantise(name, w1_codes[name][:], w1_scales[name][:])
 
         def quantise(key, codes, scales):
             nc.vector.quantize_mx(out=codes.bitcast(X4), scales=scales, in_=grouped[key][:].rearrange("p n t -> p (n t)"))
@@ -135,15 +149,17 @@ def tile_sanamixffndepthwiseglu_kernel(tc, x, w1_bytes, w1_scale, b1, wd, gain, 
             grouped[key] = dst
 
         pf = const.tile([P, 2, P], F32, name="pf")
-        nc.vector.tensor_copy(out=pf[:], in_=praw[:])
-        pbank = bank(2)
-        for h in range(2):
-            nc.tensor.transpose(pbank[:, P * h : P * (h + 1)], pf[:, h, :], ident[:])
         par = const.tile([P, 2 * P], F32, name="par")
-        nc.vector.tensor_copy(out=par[:], in_=pbank[:, 0 : 2 * P])
         wg = const.tile([P, 9, 8], F32, name="wg")
-        for tap in range(9):
-            nc.gpsimd.tensor_tensor(out=wg[:, tap, :], in0=par[:, 16 * tap : 16 * tap + 8], in1=par[:, 160:168], op=ALU.mult)
+
+        def parameters():
+            nc.vector.tensor_copy(out=pf[:], in_=praw[:])
+            pbank = bank(2)
+            for h in range(2):
+                nc.tensor.transpose(pbank[:, P * h : P * (h + 1)], pf[:, h, :], ident[:])
+            nc.vector.tensor_copy(out=par[:], in_=pbank[:, 0 : 2 * P])
+            for tap in range(9):
+                nc.gpsimd.tensor_tensor(out=wg[:, tap, :], in0=par[:, 16 * tap : 16 * tap + 8], in1=par[:, 160:168], op=ALU.mult)
 
         def weight(tap, c):
             if c < 8:
@@ -153,20 +169,33 @@ def tile_sanamixffndepthwiseglu_kernel(tc, x, w1_bytes, w1_scale, b1, wd, gain, 
         def bias(c):
             return par[:, 144 + c : 145 + c]
 
-        for t in range(4):
-            widen(2, t, "s")
-        for q in range(4):
+        def x_quantise(q):
+            quantise("x%d" % q, x_codes[:, 256 * q : 256 * (q + 1)], x_scales[:, 256 * q : 256 * (q + 1)])
+
+        def x_transposes(q):
             word_transposes("x%d" % q, [x_sb[q][:, j, :] for j in range(2)], 4 + q)
-        interleave("w2c", planes[2][:], "v")
+
+        x_transposes(0)
+        for t in range(4):
+            widen("b0", t, "s")
         word_copy("x0", "v")
-        quantise("w2c", w1_codes[2][:], w1_scales[2][:])
+        x_transposes(1)
+        parameters()
+        w1_interleave("b0", "v")
         word_copy("x1", "s")
-        word_copy("x2", "v")
-        for q in range(2):
-            quantise("x%d" % q, x_codes[:, 256 * q : 256 * (q + 1)], x_scales[:, 256 * q : 256 * (q + 1)])
+        x_quantise(0)
+        x_transposes(2)
+        w1_quantise("b0")
+        word_copy("x2", "s")
+        x_quantise(1)
+        x_transposes(3)
         word_copy("x3", "s")
-        for q in range(2, 4):
-            quantise("x%d" % q, x_codes[:, 256 * q : 256 * (q + 1)], x_scales[:, 256 * q : 256 * (q + 1)])
+        x_quantise(2)
+        x_quantise(3)
+        for t in range(4):
+            widen("a0", t, "v")
+        w1_interleave("a0", "v")
+        w1_quantise("a0")
 
         h_banks = {}
         c_banks = {}
@@ -179,15 +208,21 @@ def tile_sanamixffndepthwiseglu_kernel(tc, x, w1_bytes, w1_scale, b1, wd, gain, 
         def channel_tile(i):
             return i // 2 + (8 if i % 2 == 0 else 0)
 
+        def w1_chunk(c):
+            half = "a" if c < 8 else "b"
+            k = c % 8
+            if k < 4:
+                return half + str(k // 2), P * (k % 2)
+            return half + "2", P * (k - 4)
+
         def stage1(i):
-            c = channel_tile(i)
-            lo = P * (c % 4)
+            name, lo = w1_chunk(channel_tile(i))
             h_banks[i] = [bank(0), bank(1)]
             for hh in range(2):
                 nc.tensor.matmul_mx(
                     out=h_banks[i][hh][:],
-                    lhsT=w1_codes[c // 4][:, lo : lo + P].bitcast(X4),
-                    lhsT_scale=w1_scales[c // 4][:, lo : lo + P],
+                    lhsT=w1_codes[name][:, lo : lo + P].bitcast(X4),
+                    lhsT_scale=w1_scales[name][:, lo : lo + P],
                     rhs=x_codes[:, 512 * hh : 512 * (hh + 1)].bitcast(X4),
                     rhs_scale=x_scales[:, 512 * hh : 512 * (hh + 1)],
                     start=True,
@@ -216,61 +251,58 @@ def tile_sanamixffndepthwiseglu_kernel(tc, x, w1_bytes, w1_scale, b1, wd, gain, 
 
             return src, c
 
-        def n_scalar(i):
-            return 3 if i % 2 == 0 else 4
+        def config(i):
+            return CONFIG[i % len(CONFIG)]
 
-        def products(i):
+        def products(i, half=None):
             src, c = taps_of(i)
-            n = 9 - MERGES
-            tiles = [work.tile([P, TOK], F32, name="grp%d" % k, tag="grp%d" % k) for k in range(n)]
-            views = [t[:].rearrange("p (r c) -> p r c", c=GRID) for t in tiles]
-            groups[i] = tiles
-            ns = n_scalar(i)
+            merges, ns = config(i)
+            n = 9 - merges
+            if half in (None, 0):
+                groups[i] = [work.tile([P, TOK], F32, name="grp%d" % k, tag="grp%d" % k, bufs=3) for k in range(n)]
+            rs = slice(0, GRID) if half is None else slice(16 * half, 16 * half + 16)
+            views = [t[:].rearrange("p (r c) -> p r c", c=GRID)[:, rs, :] for t in groups[i]]
             for k in range(n - ns, n):
-                tap = k + MERGES
-                nc.scalar.activation(out=views[k], in_=src(tap), func=ACT.Copy, scale=weight(tap, c))
-            for k in range(MERGES):
-                nc.vector.tensor_scalar(out=views[k], in0=src(2 * k), scalar1=weight(2 * k, c), scalar2=None, op0=ALU.mult)
-            for k in range(MERGES):
+                tap = k + merges
+                nc.scalar.activation(out=views[k], in_=src(tap)[:, rs, :], func=ACT.Copy, scale=weight(tap, c))
+            for k in range(merges, n - ns):
+                tap = k + merges
+                nc.vector.tensor_scalar(out=views[k], in0=src(tap)[:, rs, :], scalar1=weight(tap, c), scalar2=None, op0=ALU.mult)
+            for k in range(merges):
+                nc.vector.tensor_scalar(out=views[k], in0=src(2 * k)[:, rs, :], scalar1=weight(2 * k, c), scalar2=None, op0=ALU.mult)
+            for k in range(merges):
                 tap = 2 * k + 1
-                nc.vector.scalar_tensor_tensor(out=views[k], in0=src(tap), scalar=weight(tap, c), in1=views[k], op0=ALU.mult, op1=ALU.add)
-            for k in range(MERGES, n - ns):
-                tap = k + MERGES
-                nc.vector.tensor_scalar(out=views[k], in0=src(tap), scalar1=weight(tap, c), scalar2=None, op0=ALU.mult)
+                nc.vector.scalar_tensor_tensor(out=views[k], in0=src(tap)[:, rs, :], scalar=weight(tap, c), in1=views[k], op0=ALU.mult, op1=ALU.add)
 
-        def conv(i):
-            base = 2 if i % 2 == 0 else 4
-            c_banks[i] = [bank(base), bank(base + 1)]
+        def conv(i, hh, js=(0, 1, 2, 3)):
+            if js[0] == 0:
+                c_banks[(i, hh)] = bank((2 if i % 2 == 0 else 4) + hh)
             tiles = groups[i]
-            for hh in range(2):
-                for j in range(4):
-                    tok = (4 * hh + j) * P
-                    for k in range(len(tiles)):
-                        nc.tensor.matmul(
-                            out=c_banks[i][hh][:, P * j : P * (j + 1)],
-                            lhsT=tiles[k][:, tok : tok + P],
-                            rhs=ident[:],
-                            is_transpose=True,
-                            start=(k == 0),
-                            stop=(k == len(tiles) - 1),
-                        )
-
-        def epilogue(i):
-            if i % 2 == 0:
-                gate[i // 2] = []
-                for hh in range(2):
-                    s = work.tile([P, 512], F32, name="gate%d" % hh, tag="gate%d" % hh)
-                    nc.scalar.activation(out=s[:], in_=c_banks[i][hh][:], func=ACT.Silu)
-                    gate[i // 2].append(s)
-            else:
-                k = i // 2
-                for hh in range(2):
-                    nc.vector.tensor_tensor(
-                        out=g_sb[:, 4 * hh : 4 * hh + 4, P * k : P * (k + 1)],
-                        in0=c_banks[i][hh][:].rearrange("p (j c) -> p j c", c=P),
-                        in1=gate[k][hh][:].rearrange("p (j c) -> p j c", c=P),
-                        op=ALU.mult,
+            for j in js:
+                tok = (4 * hh + j) * P
+                for k in range(len(tiles)):
+                    nc.tensor.matmul(
+                        out=c_banks[(i, hh)][:, P * j : P * (j + 1)],
+                        lhsT=tiles[k][:, tok : tok + P],
+                        rhs=ident[:],
+                        is_transpose=True,
+                        start=(k == 0),
+                        stop=(k == len(tiles) - 1),
                     )
+
+        def gate_silu(i, hh):
+            s = work.tile([P, 512], F32, name="gate%d" % hh, tag="gate%d" % hh)
+            nc.scalar.activation(out=s[:], in_=c_banks[(i, hh)][:], func=ACT.Silu)
+            gate[(i // 2, hh)] = s
+
+        def gate_product(i, hh):
+            k = i // 2
+            nc.vector.tensor_tensor(
+                out=g_sb[:, 4 * hh : 4 * hh + 4, P * k : P * (k + 1)],
+                in0=c_banks[(i, hh)][:].rearrange("p (j c) -> p j c", c=P),
+                in1=gate[(k, hh)][:].rearrange("p (j c) -> p j c", c=P),
+                op=ALU.mult,
+            )
 
         def g_transposes(jj, q, b):
             word_transposes("g%d_%d" % (jj, q), [g_sb[:, 2 * jj + j, 512 * q : 512 * (q + 1)] for j in range(2)], b)
@@ -281,60 +313,48 @@ def tile_sanamixffndepthwiseglu_kernel(tc, x, w1_bytes, w1_scale, b1, wd, gain, 
         w2_codes = [const.tile([P, D], U32, name="w2_codes%d" % q, align_bytes=64) for q in range(2)]
         w2_scales = [const.tile([P, D], U8, name="w2_scales%d" % q, align_bytes=64) for q in range(2)]
 
+        def g_word_copy(jj, q, engine):
+            word_copy("g%d_%d" % (jj, q), engine)
+
         stage1(0)
         silu_u(0)
-        for t in range(4):
-            widen(0, t, "v")
-        interleave("w0c", planes[0][:], "v")
-        quantise("w0c", w1_codes[0][:], w1_scales[0][:])
-        products(0)
         stage1(1)
         silu_u(1)
-        for i in range(N_TILES):
-            if i + 2 < N_TILES:
-                stage1(i + 2)
-            if 9 <= i and i % 2 == 1:
-                g_transposes((i - 9) // 2, 0, 6 + ((i - 9) // 2) % 2)
-            if i >= 1:
-                epilogue(i - 1)
-            if 10 <= i and i % 2 == 0:
-                g_quantise((i - 10) // 2, 0)
-            if i + 2 < N_TILES:
-                silu_u(i + 2)
-            if i + 1 < N_TILES:
-                products(i + 1)
-            if i == 1:
+        stage1(2)
+        products(0)
+        fill_w1 = {0: "b1", 1: "a1", 3: "b2", 4: "a2"}
+        for i in range(N_TILES - 3):
+            if 9 <= i:
+                g_transposes(i - 9, 0, 6 + i % 2)
+            silu_u(i + 2)
+            if i % 2 == 1:
+                for hh in range(2):
+                    gate_silu(i - 1, hh)
+            if 10 <= i:
+                g_quantise(i - 10, 0)
+            if i in fill_w1:
                 for t in range(4):
-                    widen(3, t, "s")
-            if i == 2:
-                interleave("w3c", planes[3][:], "v")
-            if i == 3:
-                quantise("w3c", w1_codes[3][:], w1_scales[3][:])
-                for t in range(4):
-                    widen(1, t, "s")
-            if i == 4:
-                interleave("w1c", planes[1][:], "v")
-            if i == 5:
-                quantise("w1c", w1_codes[1][:], w1_scales[1][:])
+                    widen(fill_w1[i], t, WIDEN[t])
+                w1_interleave(fill_w1[i], "v")
+                w1_quantise(fill_w1[i])
+            products(i + 1)
+            if i >= 2 and i % 2 == 0:
+                for hh in range(2):
+                    gate_product(i - 1, hh)
+            if i == 5 or i == 7:
+                interleave("v%d" % ((i - 5) // 2), w2_sb[(i - 5) // 2][:], "v")
             if i == 6 or i == 8:
-                interleave("v%d" % ((i - 6) // 2), w2_sb[(i - 6) // 2][:], "v")
-            if i == 7 or i == 9:
-                q = (i - 7) // 2
+                q = (i - 6) // 2
                 quantise("v%d" % q, w2_codes[q][:], w2_scales[q][:])
-            if 9 <= i and i % 2 == 1:
-                word_copy("g%d_%d" % ((i - 9) // 2, 0), "s")
-            conv(i)
-        epilogue(N_TILES - 1)
-        g_quantise(3, 0)
+            if 9 <= i:
+                g_word_copy(i - 9, 0, "s")
+            conv(i, 0)
+            stage1(i + 3)
+            conv(i, 1)
 
         out_view = out.rearrange("b h w d -> (b h w) d")
-        for jj in range(4):
-            g_transposes(jj, 1, 4 + jj)
-        for jj in range(4):
-            word_copy("g%d_1" % jj, "s" if jj % 2 else "v")
-        for jj in range(4):
-            g_quantise(jj, 1)
-        for j in range(8):
+
+        def project(j, engine):
             acc = bank(j % 4)
             for q in range(2):
                 nc.tensor.matmul_mx(
@@ -346,9 +366,50 @@ def tile_sanamixffndepthwiseglu_kernel(tc, x, w1_bytes, w1_scale, b1, wd, gain, 
                     start=(q == 0),
                     stop=(q == 1),
                 )
-            res = work.tile([P, D], F32, name="res", tag="res", bufs=4)
-            if j % 2 == 0:
+            res = const.tile([P, D], F32, name="res%d" % j, tag="io%d" % j)
+            if engine == "s":
                 nc.scalar.copy(out=res[:], in_=acc[:])
             else:
                 nc.vector.tensor_copy(out=res[:], in_=acc[:])
             nc.sync.dma_start(out=out_view[P * j : P * (j + 1), :], in_=res[:])
+
+        silu_u(15)
+        for hh in range(2):
+            gate_silu(12, hh)
+        g_quantise(3, 0)
+        products(14, 0)
+        conv(13, 0)
+        conv(13, 1)
+        products(15, 0)
+        conv(14, 0)
+        for hh in range(2):
+            gate_product(13, hh)
+        products(14, 1)
+        gate_silu(14, 0)
+        conv(15, 0)
+        conv(14, 1)
+        gate_product(15, 0)
+        g_transposes(0, 1, 6)
+        g_transposes(1, 1, 7)
+        products(15, 1)
+        g_word_copy(0, 1, "s")
+        g_word_copy(1, 1, "v")
+        gate_silu(14, 1)
+        g_quantise(0, 1)
+        g_quantise(1, 1)
+        conv(15, 1)
+        gate_product(15, 1)
+        project(0, "s")
+        project(1, "s")
+        g_transposes(2, 1, 6)
+        g_transposes(3, 1, 7)
+        g_word_copy(2, 1, "v")
+        g_word_copy(3, 1, "s")
+        g_quantise(2, 1)
+        project(2, "v")
+        g_quantise(3, 1)
+        project(3, "s")
+        project(4, "v")
+        project(5, "s")
+        project(6, "v")
+        project(7, "s")

from contextlib import ExitStack

import concourse.mybir as mybir
from concourse.masks import make_identity

P = 128
TOK = 1024
GRID = 32
D = 512
F = 1024
F2 = 2 * F

F32 = mybir.dt.float32
BF16 = mybir.dt.bfloat16
U32 = mybir.dt.uint32
U8 = mybir.dt.uint8
FP8 = mybir.dt.float8_e4m3fn
X4 = mybir.dt.float8_e4m3fn_x4
ACT = mybir.ActivationFunctionType
ALU = mybir.AluOpType

FLOPS = 2 * TOK * D * F2 + 2 * TOK * F * D + 2 * 9 * TOK * F2 + 3 * TOK * F

N_TILES = F2 // P
WIDEN = "vvvv"
PITCH = 40
COL0 = 4
CONFIG = ((2, 3), (2, 4))


def tile_sanamixffndepthwiseglu_kernel(tc, x, w1_bytes, w1_scale, b1, wd, gain, w2, out):
    nc = tc.nc
    with ExitStack() as ctx:
        const = ctx.enter_context(tc.tile_pool(name="const", bufs=1))
        work = ctx.enter_context(tc.tile_pool(name="work", bufs=2))
        psum = ctx.enter_context(tc.psum_pool(name="psum", bufs=1))
        ctx.enter_context(tc.manual_schedule())

        def bank(i):
            return psum.tile([P, 512], F32, name="bank%d" % i, tag="bank%d" % i)

        x_view = x.rearrange("b h w d -> (b h w) d").rearrange("(q j p) d -> q p j d", j=2, p=P)
        w1_view = w1_bytes.rearrange("(p t) n -> p t n", t=4)
        w2_view = w2.rearrange("(q p t) n -> q p t n", p=P, t=4)

        ident = const.tile([P, P], F32, name="ident")
        make_identity(nc, ident[:])
        u_bufs = []
        for i in range(3):
            u = const.tile([P, GRID + 2, PITCH], F32, name="u%d" % i)
            nc.gpsimd.memset(u[:], 0.0)
            u_bufs.append(u)

        praw = const.tile([P, 2, P], BF16, name="praw")
        nc.vector.memset(praw[:, 1, :], 0.0)
        warm = const.tile([P, 1], F32, name="warm")
        nc.vector.memset(warm[:], 0.0)
        nc.scalar.activation(out=warm[:], in_=warm[:], func=ACT.Silu)

        x_sb = [const.tile([P, 2, D], BF16, name="x_sb%d" % q, tag="io%d" % q) for q in range(4)]
        w1_sb = [const.tile([P, 4, 512], U8, name="w1_sb%d" % c, tag="io%d" % (4 + c)) for c in range(4)]
        w2_sb = [const.tile([P, 4, D], BF16, name="w2_sb%d" % q) for q in range(2)]
        scale_sb = const.tile([P, 4], F32, name="scale_sb")

        def load_x(q):
            nc.sync.dma_start(out=x_sb[q][:], in_=x_view[q])

        def load_w1(c):
            nc.sync.dma_start(out=w1_sb[c][:], in_=w1_view[:, :, 512 * c : 512 * (c + 1)])

        nc.scalar.dma_start(out=scale_sb[:], in_=w1_scale.rearrange("(p t) o -> p (t o)", t=4))
        wd_rows = wd.rearrange("r t (c p) -> (r t c) p", p=P)
        nc.scalar.dma_start(out=praw[:, 0, :], in_=wd_rows[0:128, :])
        nc.scalar.dma_start(out=praw[0:16, 1, :], in_=wd_rows[128:144, :])
        nc.scalar.dma_start(out=praw[16:32, 1, :], in_=b1.rearrange("(c p) -> c p", p=P))
        nc.scalar.dma_start(out=praw[32:40, 1, :], in_=gain.rearrange("(c p) -> c p", p=P))
        load_x(0)
        load_w1(2)
        load_x(1)
        load_x(2)
        load_x(3)
        load_w1(0)
        load_w1(3)
        load_w1(1)
        for q in range(2):
            nc.sync.dma_start(out=w2_sb[q][:], in_=w2_view[q])

        chunks = {"b0": (2, 0, 256), "b1": (2, 256, 256), "b2": (3, 0, 512), "a0": (0, 0, 256), "a1": (0, 256, 256), "a2": (1, 0, 512)}
        w1_codes = {}
        w1_scales = {}
        for name in chunks:
            width = chunks[name][2]
            w1_codes[name] = const.tile([P, width], U32, name="w1_codes_" + name, align_bytes=64)
            w1_scales[name] = const.tile([P, width], U8, name="w1_scales_" + name, align_bytes=64)
        planes = {}
        grouped = {}

        def widen(name, t, engine):
            c, lo, width = chunks[name]
            if t == 0:
                planes[name] = work.tile([P, 4, width], BF16, name="planes%d" % width, tag="planes%d" % width, align_bytes=64)
            src = w1_sb[c][:, t, lo : lo + width].bitcast(FP8)
            dst = planes[name][:, t, :]
            if engine == "s":
                nc.scalar.activation(out=dst, in_=src, func=ACT.Copy, scale=scale_sb[:, t : t + 1])
            else:
                nc.vector.tensor_scalar(out=dst, in0=src, scalar1=scale_sb[:, t : t + 1], scalar2=None, op0=ALU.mult)

        def interleave(key, src, engine):
            width = src.shape[2]
            dst = work.tile([P, width, 4], BF16, name="grouped%d" % width, tag="grouped%d" % width, align_bytes=64)
            grouped[key] = dst
            view = src.rearrange("p t n -> p n t")
            if engine == "s":
                nc.scalar.copy(out=dst[:], in_=view)
            else:
                nc.vector.tensor_copy(out=dst[:], in_=view)

        def w1_interleave(name, engine):
            interleave(name, planes[name][:], engine)

        def w1_quantise(name):
            quantise(name, w1_codes[name][:], w1_scales[name][:])

        def quantise(key, codes, scales):
            nc.vector.quantize_mx(out=codes.bitcast(X4), scales=scales, in_=grouped[key][:].rearrange("p n t -> p (n t)"))

        x_codes = const.tile([P, TOK], U32, name="x_codes", align_bytes=64)
        x_scales = const.tile([P, TOK], U8, name="x_scales", align_bytes=64)
        pair_tiles = {}

        def word_transposes(key, sources, b):
            tx = bank(b)
            for j in range(2):
                words = sources[j].bitcast(F32)
                for h in range(2):
                    col = (2 * j + h) * P
                    nc.tensor.transpose(tx[:, col : col + P], words[:, h:256:2], ident[:])
            pair_tiles[key] = tx

        def word_copy(key, engine):
            dst = work.tile([P, 256, 4], BF16, name="pairs", tag="pairs", bufs=4, align_bytes=64)
            o = dst[:].rearrange("p n t -> p (n t)").bitcast(F32).rearrange("p (j r h) -> p j r h", j=2, h=2)
            i = pair_tiles[key][:].rearrange("p (j h r) -> p j r h", j=2, h=2)
            if engine == "s":
                nc.scalar.copy(out=o, in_=i)
            else:
                nc.vector.tensor_copy(out=o, in_=i)
            grouped[key] = dst

        pf = const.tile([P, 2, P], F32, name="pf")
        par = const.tile([P, 2 * P], F32, name="par")
        wg = const.tile([P, 9, 8], F32, name="wg")

        def parameters():
            nc.vector.tensor_copy(out=pf[:], in_=praw[:])
            pbank = bank(2)
            for h in range(2):
                nc.tensor.transpose(pbank[:, P * h : P * (h + 1)], pf[:, h, :], ident[:])
            nc.vector.tensor_copy(out=par[:], in_=pbank[:, 0 : 2 * P])
            for tap in range(9):
                nc.gpsimd.tensor_tensor(out=wg[:, tap, :], in0=par[:, 16 * tap : 16 * tap + 8], in1=par[:, 160:168], op=ALU.mult)

        def weight(tap, c):
            if c < 8:
                return wg[:, tap, c : c + 1]
            return par[:, 16 * tap + c : 16 * tap + c + 1]

        def bias(c):
            return par[:, 144 + c : 145 + c]

        def x_quantise(q):
            quantise("x%d" % q, x_codes[:, 256 * q : 256 * (q + 1)], x_scales[:, 256 * q : 256 * (q + 1)])

        def x_transposes(q):
            word_transposes("x%d" % q, [x_sb[q][:, j, :] for j in range(2)], 4 + q)

        x_transposes(0)
        for t in range(4):
            widen("b0", t, "s")
        word_copy("x0", "v")
        x_transposes(1)
        parameters()
        w1_interleave("b0", "v")
        word_copy("x1", "s")
        x_quantise(0)
        x_transposes(2)
        w1_quantise("b0")
        word_copy("x2", "s")
        x_quantise(1)
        x_transposes(3)
        word_copy("x3", "s")
        x_quantise(2)
        x_quantise(3)
        for t in range(4):
            widen("a0", t, "v")
        w1_interleave("a0", "v")
        w1_quantise("a0")

        h_banks = {}
        c_banks = {}
        groups = {}
        gate = {}
        g_sb = const.tile([P, 8, F], BF16, name="g_sb", align_bytes=64)
        g_codes = [const.tile([P, TOK], U32, name="g_codes%d" % q, align_bytes=64) for q in range(2)]
        g_scales = [const.tile([P, TOK], U8, name="g_scales%d" % q, align_bytes=64) for q in range(2)]

        def channel_tile(i):
            return i // 2 + (8 if i % 2 == 0 else 0)

        def w1_chunk(c):
            half = "a" if c < 8 else "b"
            k = c % 8
            if k < 4:
                return half + str(k // 2), P * (k % 2)
            return half + "2", P * (k - 4)

        def stage1(i):
            name, lo = w1_chunk(channel_tile(i))
            h_banks[i] = [bank(0), bank(1)]
            for hh in range(2):
                nc.tensor.matmul_mx(
                    out=h_banks[i][hh][:],
                    lhsT=w1_codes[name][:, lo : lo + P].bitcast(X4),
                    lhsT_scale=w1_scales[name][:, lo : lo + P],
                    rhs=x_codes[:, 512 * hh : 512 * (hh + 1)].bitcast(X4),
                    rhs_scale=x_scales[:, 512 * hh : 512 * (hh + 1)],
                    start=True,
                    stop=True,
                )

        def silu_u(i):
            c = channel_tile(i)
            u = u_bufs[i % 3]
            for hh in range(2):
                nc.scalar.activation(
                    out=u[:, 1 + 16 * hh : 17 + 16 * hh, COL0 : COL0 + GRID],
                    in_=h_banks[i][hh][:].rearrange("p (r c) -> p r c", c=GRID),
                    func=ACT.Silu,
                    bias=bias(c),
                    scale=1.0,
                )

        def taps_of(i):
            u = u_bufs[i % 3]
            c = channel_tile(i)

            def src(tap):
                r, t = divmod(tap, 3)
                return u[:, r : r + GRID, COL0 - 1 + t : COL0 - 1 + t + GRID]

            return src, c

        def config(i):
            return CONFIG[i % len(CONFIG)]

        def products(i, half=None):
            src, c = taps_of(i)
            merges, ns = config(i)
            n = 9 - merges
            if half in (None, 0):
                groups[i] = [work.tile([P, TOK], F32, name="grp%d" % k, tag="grp%d" % k, bufs=3) for k in range(n)]
            rs = slice(0, GRID) if half is None else slice(16 * half, 16 * half + 16)
            views = [t[:].rearrange("p (r c) -> p r c", c=GRID)[:, rs, :] for t in groups[i]]
            for k in range(n - ns, n):
                tap = k + merges
                nc.scalar.activation(out=views[k], in_=src(tap)[:, rs, :], func=ACT.Copy, scale=weight(tap, c))
            for k in range(merges, n - ns):
                tap = k + merges
                nc.vector.tensor_scalar(out=views[k], in0=src(tap)[:, rs, :], scalar1=weight(tap, c), scalar2=None, op0=ALU.mult)
            for k in range(merges):
                nc.vector.tensor_scalar(out=views[k], in0=src(2 * k)[:, rs, :], scalar1=weight(2 * k, c), scalar2=None, op0=ALU.mult)
            for k in range(merges):
                tap = 2 * k + 1
                nc.vector.scalar_tensor_tensor(out=views[k], in0=src(tap)[:, rs, :], scalar=weight(tap, c), in1=views[k], op0=ALU.mult, op1=ALU.add)

        def conv(i, hh, js=(0, 1, 2, 3)):
            if js[0] == 0:
                c_banks[(i, hh)] = bank((2 if i % 2 == 0 else 4) + hh)
            tiles = groups[i]
            for j in js:
                tok = (4 * hh + j) * P
                for k in range(len(tiles)):
                    nc.tensor.matmul(
                        out=c_banks[(i, hh)][:, P * j : P * (j + 1)],
                        lhsT=tiles[k][:, tok : tok + P],
                        rhs=ident[:],
                        is_transpose=True,
                        start=(k == 0),
                        stop=(k == len(tiles) - 1),
                    )

        def gate_silu(i, hh):
            s = work.tile([P, 512], F32, name="gate%d" % hh, tag="gate%d" % hh)
            nc.scalar.activation(out=s[:], in_=c_banks[(i, hh)][:], func=ACT.Silu)
            gate[(i // 2, hh)] = s

        def gate_product(i, hh):
            k = i // 2
            nc.vector.tensor_tensor(
                out=g_sb[:, 4 * hh : 4 * hh + 4, P * k : P * (k + 1)],
                in0=c_banks[(i, hh)][:].rearrange("p (j c) -> p j c", c=P),
                in1=gate[(k, hh)][:].rearrange("p (j c) -> p j c", c=P),
                op=ALU.mult,
            )

        def g_transposes(jj, q, b):
            word_transposes("g%d_%d" % (jj, q), [g_sb[:, 2 * jj + j, 512 * q : 512 * (q + 1)] for j in range(2)], b)

        def g_quantise(jj, q):
            quantise("g%d_%d" % (jj, q), g_codes[q][:, 256 * jj : 256 * (jj + 1)], g_scales[q][:, 256 * jj : 256 * (jj + 1)])

        w2_codes = [const.tile([P, D], U32, name="w2_codes%d" % q, align_bytes=64) for q in range(2)]
        w2_scales = [const.tile([P, D], U8, name="w2_scales%d" % q, align_bytes=64) for q in range(2)]

        def g_word_copy(jj, q, engine):
            word_copy("g%d_%d" % (jj, q), engine)

        stage1(0)
        silu_u(0)
        stage1(1)
        silu_u(1)
        stage1(2)
        products(0)
        fill_w1 = {0: "b1", 1: "a1", 3: "b2", 4: "a2"}
        for i in range(N_TILES - 3):
            if 9 <= i:
                g_transposes(i - 9, 0, 6 + i % 2)
            silu_u(i + 2)
            if i % 2 == 1:
                for hh in range(2):
                    gate_silu(i - 1, hh)
            if 10 <= i:
                g_quantise(i - 10, 0)
            if i in fill_w1:
                for t in range(4):
                    widen(fill_w1[i], t, WIDEN[t])
                w1_interleave(fill_w1[i], "v")
                w1_quantise(fill_w1[i])
            products(i + 1)
            if i >= 2 and i % 2 == 0:
                for hh in range(2):
                    gate_product(i - 1, hh)
            if i == 5 or i == 7:
                interleave("v%d" % ((i - 5) // 2), w2_sb[(i - 5) // 2][:], "v")
            if i == 6 or i == 8:
                q = (i - 6) // 2
                quantise("v%d" % q, w2_codes[q][:], w2_scales[q][:])
            if 9 <= i:
                g_word_copy(i - 9, 0, "s")
            conv(i, 0)
            stage1(i + 3)
            conv(i, 1)

        out_view = out.rearrange("b h w d -> (b h w) d")

        def project(j, engine):
            acc = bank(j % 4)
            for q in range(2):
                nc.tensor.matmul_mx(
                    out=acc[:],
                    lhsT=g_codes[q][:, P * j : P * (j + 1)].bitcast(X4),
                    lhsT_scale=g_scales[q][:, P * j : P * (j + 1)],
                    rhs=w2_codes[q][:].bitcast(X4),
                    rhs_scale=w2_scales[q][:],
                    start=(q == 0),
                    stop=(q == 1),
                )
            res = const.tile([P, D], F32, name="res%d" % j, tag="io%d" % j)
            if engine == "s":
                nc.scalar.copy(out=res[:], in_=acc[:])
            else:
                nc.vector.tensor_copy(out=res[:], in_=acc[:])
            nc.sync.dma_start(out=out_view[P * j : P * (j + 1), :], in_=res[:])

        silu_u(15)
        for hh in range(2):
            gate_silu(12, hh)
        g_quantise(3, 0)
        products(14, 0)
        conv(13, 0)
        conv(13, 1)
        products(15, 0)
        conv(14, 0)
        for hh in range(2):
            gate_product(13, hh)
        products(14, 1)
        gate_silu(14, 0)
        conv(15, 0)
        conv(14, 1)
        gate_product(15, 0)
        g_transposes(0, 1, 6)
        g_transposes(1, 1, 7)
        products(15, 1)
        g_word_copy(0, 1, "s")
        g_word_copy(1, 1, "v")
        gate_silu(14, 1)
        g_quantise(0, 1)
        g_quantise(1, 1)
        conv(15, 1)
        gate_product(15, 1)
        project(0, "s")
        project(1, "s")
        g_transposes(2, 1, 6)
        g_transposes(3, 1, 7)
        g_word_copy(2, 1, "v")
        g_word_copy(3, 1, "s")
        g_quantise(2, 1)
        project(2, "v")
        g_quantise(3, 1)
        project(3, "s")
        project(4, "v")
        project(5, "s")
        project(6, "v")
        project(7, "s")
